import numpy as np, ml_dtypes
CORES = [1,5,17,21,33,37,49,53]
N = 8
import mx_ref
BF = ml_dtypes.bfloat16
def gentries(a):
    return np.ascontiguousarray(a.reshape(8, 16, -1).transpose(0, 2, 1)).reshape(8, -1)
def gtable(e):
    e = np.asarray(e); return np.ascontiguousarray(e.reshape(8, -1, 16).transpose(0, 2, 1)).reshape(128, -1).astype(np.int32)
def gcols(t, e):
    v = np.concatenate([t.reshape(8, 16, -1, 4), np.zeros((8, 16, 1, 4), BF)], axis=2)
    return np.ascontiguousarray(np.stack([v[g][:, e[g]] for g in range(8)])).reshape(128, -1)
def f(rng, *shape):
    return mx_ref.flush((rng.standard_normal(shape, dtype=np.float32) * np.exp2(rng.integers(-2, 3, shape[:-1] + (1,)))).astype(BF))
def wide(rng, *shape, cols=0):
    v = rng.standard_normal(shape, dtype=np.float32) * np.exp2(rng.integers(-12, 13, shape)).astype(np.float32)
    if cols: v *= np.repeat(np.exp2(rng.integers(-cols, cols + 1, shape[:-2] + (1, shape[-1] // 4))) * (rng.random(shape[:-2] + (1, shape[-1] // 4)) > 0.0625), 4, axis=-1).astype(np.float32)
    return mx_ref.flush(v.astype(BF))
T, O, K = 256, 2, 256
def lists(rng, alike=False, groups=False, ends=False, few=False):
    c = []
    for r in range(N):
        e = rng.integers(0, K, (8, O, 2, 128))
        if groups: e = np.stack([e[0]] * 8)
        if ends: e = rng.permuted(np.resize([0, K - 1], (8, O, 2, 128)), axis=3)
        if few:
            for m in range(2): e[:, :, m] = rng.permutation(np.resize(rng.permutation(K)[:8], 8 * O * 128)).reshape(8, O, 128)
        c.append(gtable(e.reshape(8, -1)))
    if alike: c = [c[0]] * N
    return np.stack(c)
def setup_inputs(rng):
    return {"x": f(rng, N, 128, 4 * T), "book": np.stack([f(rng, 128, 8 * K)] * N), "cw": lists(rng)}
def setup_inputs_alike(rng):
    d = setup_inputs(rng); d["cw"] = lists(rng, alike=True); return d
def setup_inputs_groups(rng):
    d = setup_inputs(rng); d["cw"] = lists(rng, groups=True); return d
def setup_inputs_ends(rng):
    d = setup_inputs(rng); d["cw"] = lists(rng, ends=True); return d
def setup_inputs_few(rng):
    d = setup_inputs(rng); d["cw"] = lists(rng, few=True); return d
def setup_inputs_spread(rng):
    d = setup_inputs(rng); d["x"] = wide(rng, N, 128, 4 * T, cols=8); d["book"] = np.stack([wide(rng, 128, 8 * K, cols=4)] * N); return d
def check_inputs(d):
    b = []
    for r in range(N):
        if d["cw"][r].min() < 0 or d["cw"][r].max() >= K: b.append("cw")
        if d["book"][r].tobytes() != d["book"][0].tobytes(): b.append("book")
    return b
def reference(x, book, cw):
    W = []
    for s in range(N):
        e = gentries(cw[s])
        for o in range(O):
            a, b = [gcols(np.ascontiguousarray(book[s][:, 4 * K * m:4 * K * m + 4 * K]), e[:, (2 * o + m) * 128:(2 * o + m) * 128 + 128]).astype(np.float32) for m in range(2)]
            W.append(mx_ref.quantize((a + b).astype(BF)))
    y = np.zeros((N, 128, N * O * T), np.float32)
    for r in range(N):
        X = mx_ref.quantize(np.ascontiguousarray(x[r]))
        for i in range(N * O): y[r][:, T * i:T * i + T] = mx_ref.matmul(W[i], X)
    return {"y": y}

@@ -1,0 +1,205 @@
+from concourse.bass import DstId, RemoteDMATransfer
+from concourse.mybir import dt, AluOpType, ActivationFunctionType
+
+N, O, T_COLS, K = 8, 2, 256, 256
+W = 128
+P = O * W
+BANKS = 8
+
+SCRATCH = {
+    "cwl": ("sbuf", [128, O, 2, W // 16], "int32"),
+    "bk0": ("sbuf", [128, 4 * K], "bfloat16"),
+    "bk1": ("sbuf", [128, 4 * K], "bfloat16"),
+    "xb": ("sbuf", [128, 4 * T_COLS], "bfloat16"),
+    "xq": ("sbuf", [128, T_COLS], "float8_e4m3fn_x4"),
+    "xz": ("sbuf", [128, T_COLS], "uint8"),
+    "yb": ("sbuf", [128, N * O * T_COLS], "float32"),
+}
+for _k in range(N):
+    SCRATCH["w%d" % _k] = ("sbuf", [128, P], "float8_e4m3fn_x4")
+    SCRATCH["z%d" % _k] = ("sbuf", [128, P], "uint8")
+    SCRATCH["li%d" % _k] = ("sbuf", [128, 8 * P // 16], "uint16")
+for _k in range(4):
+    SCRATCH["g%d" % _k] = ("sbuf", [128, 4 * P], "bfloat16")
+    SCRATCH["h%d" % _k] = ("sbuf", [128, 4 * P], "bfloat16")
+for _k in range(BANKS):
+    SCRATCH["ps%d" % _k] = ("psum", [128, 512], "float32")
+
+SEMAPHORES = ["s_cw", "s_b0", "s_b1", "s_x", "s_list", "s_xq", "s_sent", "s_out"]
+SEMAPHORES += ["s_g%d%d" % (i, t) for i in range(4) for t in range(4)]
+SEMAPHORES += ["s_h%d" % i for i in range(4)] + ["s_q%d" % i for i in range(4)]
+SEMAPHORES += ["s_al%d" % s for s in range(N)] + ["s_ar%d" % s for s in range(N)]
+SEMAPHORES += ["s_mm%d" % i for i in range(N * O)] + ["s_ev%d" % i for i in range(N * O)]
+
+PLAN = {
+    "lists": [2, 3], "codes": [1],
+    "tensor": ["own", "mate", "l0", "c0", "l1", "m0", "d0", "m1"],
+    "scalar": ["g own", "e own 0", "g l0", "g l1", "e mate 0", "e l0 0", "e l0 1", "e c0 0", "e c0 1", "e m0 0", "e d0 0", "e m1 0"],
+    "vector": ["a own", "x", "e own 1", "a l0", "a l1", "e mate 1", "e l1 0", "e l1 1", "e m0 1", "e d0 1", "e m1 1"],
+    "store": [["own"], ["mate"], ["l0"], ["c0"], ["l1"], ["m0"], ["d0"], ["m1"]],
+    "mate_eng": {"own": "rest", "l0": "rest", "l1": "on"},
+}
+
+
+def bits(engines):
+    return sum(1 << e for e in engines)
+
+
+def rank_program(g, core, T, topo):
+    r = T.rank_of(core)
+    if r is None:
+        return
+    cores = T.cores
+    chips = sorted(set(topo.chip(c) for c in cores))
+    here = chips.index(topo.chip(core))
+    same, other = {}, {}
+    for s, c in enumerate(cores):
+        (same if topo.die(c) == topo.die(core) else other)[chips.index(topo.chip(c))] = s
+    role = {"own": r, "mate": other[here]}
+    made = {"own": 0}
+    for k, v in enumerate(PLAN["lists"]):
+        role["l%d" % k], role["m%d" % k] = same[here ^ v], other[here ^ v]
+        made["l%d" % k] = k + 1
+    for k, v in enumerate(PLAN["codes"]):
+        role["c%d" % k], role["d%d" % k] = same[here ^ v], other[here ^ v]
+    far = cores[same[here ^ 1]]
+    sets = {"on": topo.engines(core, cores[role["mate"]]), "off": topo.engines(core, far)}
+    sets["rest"] = [e for e in sets["on"] if e not in sets["off"]]
+    off = sets["off"]
+    sent = [0]
+
+    def transfer(dst, engines, sem, src, to):
+        rid, pid = topo.addr(cores[dst])[:2]
+        sent[0] += len(engines)
+        return RemoteDMATransfer(dst_ids=[DstId(rid=rid, pnc=pid)], dma_engine_mask=bits(engines),
+                                 remote_sem=T.sem[sem], src=src, dst=to)
+
+    def send(s, ways):
+        q, z = T["w%d" % s], T["z%d" % s]
+        g.remote_dma_fused([transfer(d, e, "s_ar%d" % s, q[:, 0:P].bitcast(dt.uint8), q[:, 0:P].bitcast(dt.uint8))
+                            for d, e in ways], local_sem=T.sem.s_sent)
+        g.remote_dma_fused([transfer(d, e, "s_ar%d" % s, z[:, 0:P], z[:, 0:P]) for d, e in ways], local_sem=T.sem.s_sent)
+
+    ways, half = [], len(off) // 2
+    for k in range(len(PLAN["codes"])):
+        ways += [[(role["c%d" % k], off[:half]), (role["d%d" % k], off[half:])]]
+    arrive = {"mate": len(sets[PLAN["mate_eng"]["own"]])}
+    for k in range(len(PLAN["lists"])):
+        arrive["m%d" % k] = len(sets[PLAN["mate_eng"]["l%d" % k]])
+    for k in range(len(PLAN["codes"])):
+        arrive["c%d" % k] = arrive["d%d" % k] = half
+
+    g.sync.dma_start(T.cwl[:, :, :, :], T.cw[:, :]).then_inc(T.sem.s_cw, 16)
+    g.sync.dma_start(T.bk1[:, :], T.book[:, 4 * K:8 * K]).then_inc(T.sem.s_b1, 16)
+    g.sync.dma_start(T.bk0[:, :], T.book[:, 0:4 * K]).then_inc(T.sem.s_b0, 16)
+    g.sync.dma_start(T.xb[:, :], T.x[:, :]).then_inc(T.sem.s_x, 16)
+
+    n = P // 16
+    g.vector.wait_ge(T.sem.s_cw, 16)
+    own = T["li%d" % r]
+    for m in (1, 0):
+        for t in range(4):
+            k = (m * 4 + t) * n
+            g.vector.tensor_scalar(own[:, k:k + n], T.cwl[:, :, m, :], 4.0, float(t), AluOpType.mult,
+                                   AluOpType.add).then_inc(T.sem.s_list, 1)
+
+    nl = len(PLAN["lists"])
+    g.wait_ge(T.sem.s_list, 8)
+    for k in range(nl):
+        g.remote_dma_fused([transfer(role["l%d" % k], off, "s_al%d" % r, own[:, :], own[:, :])], local_sem=T.sem.s_sent)
+    g.wait_ge(T.sem.s_q0, 1)
+    first = [(role["mate"], sets[PLAN["mate_eng"]["own"]])]
+    if PLAN["mate_eng"]["own"] == "rest":
+        send(r, first + (ways[0] if ways else []))
+        rem = ways[1:]
+    else:
+        send(r, first)
+        rem = ways
+    for w in rem:
+        send(r, w)
+    for k in range(nl):
+        g.wait_ge(T.sem["s_q%d" % (k + 1)], 1)
+        send(role["l%d" % k], [(role["mate"], sets[PLAN["mate_eng"]["l%d" % k]])])
+    g.wait_ge(T.sem.s_sent, sent[0])
+
+    seen = {"scalar": set(), "vector": set()}
+
+    def once(name, q, sem, val):
+        if sem not in seen[name]:
+            seen[name].add(sem)
+            q.wait_ge(T.sem[sem], val)
+
+    def list_wait(name, q, who):
+        if who == "own":
+            once(name, q, "s_list", 8)
+        else:
+            once(name, q, "s_al%d" % role[who], len(off))
+
+    def evac(q, who, o):
+        i = role[who] * O + o
+        p = PLAN["tensor"].index(who) * O + o
+        q.wait_ge(T.sem["s_mm%d" % i], 1)
+        src, to = T["ps%d" % (p % BANKS)][:, 0:T_COLS], T.yb[:, i * T_COLS:(i + 1) * T_COLS]
+        if q is g.scalar:
+            c = q.activation(to, src, ActivationFunctionType.Copy)
+        else:
+            c = q.tensor_copy(to, src)
+        c.then_inc(T.sem["s_ev%d" % i], 1)
+
+    for op in PLAN["scalar"]:
+        op = op.split()
+        if op[0] == "e":
+            evac(g.scalar, op[1], int(op[2]))
+            continue
+        i, off16 = made[op[1]], T["li%d" % role[op[1]]]
+        once("scalar", g.scalar, "s_b1", 16)
+        list_wait("scalar", g.scalar, op[1])
+        for t in range(4):
+            k = (4 + t) * n
+            g.scalar.activation(T["g%d" % i][:, t:4 * P:4], T.bk1[:, 0:4 * K].indirect(off16[:, k:k + n]),
+                                ActivationFunctionType.Copy).then_inc(T.sem["s_g%d%d" % (i, t)], 1)
+
+    for op in PLAN["vector"]:
+        op = op.split()
+        if op[0] == "e":
+            evac(g.vector, op[1], int(op[2]))
+        elif op[0] == "x":
+            g.vector.wait_ge(T.sem.s_x, 16)
+            g.vector.quantize_mx(T.xq[:, 0:T_COLS], T.xz[:, 0:T_COLS], T.xb[:, 0:4 * T_COLS]).then_inc(T.sem.s_xq, 1)
+        else:
+            i, s = made[op[1]], role[op[1]]
+            once("vector", g.vector, "s_b0", 16)
+            list_wait("vector", g.vector, op[1])
+            for t in range(4):
+                k = t * n
+                g.vector.wait_ge(T.sem["s_g%d%d" % (i, t)], 1)
+                g.vector.tensor_tensor(T["h%d" % i][:, t:4 * P:4], T.bk0[:, 0:4 * K].indirect(T["li%d" % s][:, k:k + n]),
+                                       T["g%d" % i][:, t:4 * P:4], AluOpType.add).then_inc(T.sem["s_h%d" % i], 1)
+            g.vector.wait_ge(T.sem["s_h%d" % i], 4)
+            g.vector.quantize_mx(T["w%d" % s][:, 0:P], T["z%d" % s][:, 0:P],
+                                 T["h%d" % i][:, 0:4 * P]).then_inc(T.sem["s_q%d" % i], 1)
+
+    order = [(w, o) for w in PLAN["tensor"] for o in range(O)]
+    g.tensor.wait_ge(T.sem.s_xq, 1)
+    for p, (who, o) in enumerate(order):
+        s = role[who]
+        if o == 0:
+            if who in made:
+                g.tensor.wait_ge(T.sem["s_q%d" % made[who]], 1)
+            else:
+                g.tensor.wait_ge(T.sem["s_ar%d" % s], 2 * arrive[who])
+        if p >= BANKS:
+            pw, po = order[p - BANKS]
+            g.tensor.wait_ge(T.sem["s_ev%d" % (role[pw] * O + po)], 1)
+        g.tensor.matmul_mx(T["ps%d" % (p % BANKS)][:, 0:T_COLS], T["w%d" % s][:, o * W:(o + 1) * W],
+                           T["z%d" % s][:, o * W:(o + 1) * W], T.xq[:, 0:T_COLS], T.xz[:, 0:T_COLS],
+                           True, True).then_inc(T.sem["s_mm%d" % (s * O + o)], 1)
+
+    for group in PLAN["store"]:
+        ss = sorted(role[w] for w in group)
+        for s in ss:
+            for o in range(O):
+                g.sync.wait_ge(T.sem["s_ev%d" % (s * O + o)], 1)
+        a, b = ss[0] * O * T_COLS, (ss[-1] + 1) * O * T_COLS
+        g.sync.dma_start(T.y[:, a:b], T.yb[:, a:b]).then_inc(T.sem.s_out, 16)
+    g.sync.wait_ge(T.sem.s_out, 16 * len(PLAN["store"]))

@@ -5,9 +5,11 @@ N, O, T_COLS, K = 8, 2, 256, 256
 W = 128
 P = O * W
 BANKS = 8
+LC = W // 16
+SLOTS = 4
 
 SCRATCH = {
-    "cwl": ("sbuf", [128, O, 2, W // 16], "int32"),
+    "cwl": ("sbuf", [128, O, 2, LC], "int32"),
     "bk0": ("sbuf", [128, 4 * K], "bfloat16"),
     "bk1": ("sbuf", [128, 4 * K], "bfloat16"),
     "xb": ("sbuf", [128, 4 * T_COLS], "bfloat16"),
@@ -18,26 +20,27 @@ SCRATCH = {
 for _k in range(N):
     SCRATCH["w%d" % _k] = ("sbuf", [128, P], "float8_e4m3fn_x4")
     SCRATCH["z%d" % _k] = ("sbuf", [128, P], "uint8")
-    SCRATCH["li%d" % _k] = ("sbuf", [128, 8 * P // 16], "uint16")
-for _k in range(4):
+    SCRATCH["li%d" % _k] = ("sbuf", [128, 8 * O * LC], "uint16")
+for _k in range(SLOTS):
     SCRATCH["g%d" % _k] = ("sbuf", [128, 4 * P], "bfloat16")
     SCRATCH["h%d" % _k] = ("sbuf", [128, 4 * P], "bfloat16")
 for _k in range(BANKS):
     SCRATCH["ps%d" % _k] = ("psum", [128, 512], "float32")
 
-SEMAPHORES = ["s_cw", "s_b0", "s_b1", "s_x", "s_list", "s_xq", "s_sent", "s_out"]
-SEMAPHORES += ["s_g%d%d" % (i, t) for i in range(4) for t in range(4)]
-SEMAPHORES += ["s_h%d" % i for i in range(4)] + ["s_q%d" % i for i in range(4)]
-SEMAPHORES += ["s_al%d" % s for s in range(N)] + ["s_ar%d" % s for s in range(N)]
-SEMAPHORES += ["s_mm%d" % i for i in range(N * O)] + ["s_ev%d" % i for i in range(N * O)]
+SEMAPHORES = ["s_cw", "s_b0", "s_b1", "s_x", "s_l0", "s_l1", "s_xq", "s_sent", "s_out"]
+SEMAPHORES += ["s_g%d%d%d" % (i, o, t) for i in range(SLOTS) for o in range(O) for t in range(4)]
+SEMAPHORES += ["s_h%d%d" % (i, o) for i in range(SLOTS) for o in range(O)]
+SEMAPHORES += ["s_al%d" % s for s in range(N)]
+SEMAPHORES += ["s_%s%d" % (k, i) for k in ("q", "ar", "mm", "ev") for i in range(N * O)]
 
 PLAN = {
-    "lists": [2, 3], "codes": [1],
-    "tensor": ["own", "mate", "l0", "c0", "l1", "m0", "d0", "m1"],
-    "scalar": ["g own", "e own 0", "g l0", "g l1", "e mate 0", "e l0 0", "e l0 1", "e c0 0", "e c0 1", "e m0 0", "e d0 0", "e m1 0"],
-    "vector": ["a own", "x", "e own 1", "a l0", "a l1", "e mate 1", "e l1 0", "e l1 1", "e m0 1", "e d0 1", "e m1 1"],
-    "store": [["own"], ["mate"], ["l0"], ["c0"], ["l1"], ["m0"], ["d0"], ["m1"]],
-    "mate_eng": {"own": "rest", "l0": "rest", "l1": "on"},
+    "remote": ["L o>b:off", "L o>c:off", "S o0>m:rest o0>a:off", "S o1>m:rest o1>a:off", "S b>m:all", "S a>m:all",
+               "S c>m:all"],
+    "tensor": "o0 o1 m0 m1 b0 b1 a0 a1 B0 B1 c0 c1 A0 A1 C0 C1",
+    "scalar": ["g o 01", "g b 01", "e o0", "g b 23", "e o1", "g c 01", "e m0", "g c 23", "e m1", "e b0", "e b1", "e a0",
+               "e a1", "e B0", "e c0", "e A0", "e C0"],
+    "vector": ["g o 23", "a o0 2301", "x", "a o1 0123", "a b 0123", "a c 0123", "e B1", "e c1", "e A1", "e C1"],
+    "store": ["o0", "o1", "m", "b", "a", "B", "c", "A", "C"],
 }
 
 
@@ -45,161 +48,177 @@ def bits(engines):
     return sum(1 << e for e in engines)
 
 
+def roles(rank, cores, topo):
+    chips = sorted(set(topo.chip(c) for c in cores))
+    here, die = chips.index(topo.chip(cores[rank])), topo.die(cores[rank])
+    role = {}
+    for s, c in enumerate(cores):
+        role[("oabc" if topo.die(c) == die else "mABC")[chips.index(topo.chip(c)) ^ here]] = s
+    return role
+
+
+def engine_sets(core, near, far, topo):
+    on, off = topo.engines(core, near), topo.engines(core, far)
+    rest = [e for e in on if e not in off]
+    h = len(off) // 2
+    return {"all": on, "off": off, "rest": rest, "off0": off[:h], "off1": off[h:], "rest0": rest[:h], "rest1": rest[h:]}
+
+
+def tiles_of(item):
+    return [int(item[1])] if len(item) > 1 else list(range(O))
+
+
+def remote_steps(rank, cores, topo):
+    role = roles(rank, cores, topo)
+    sets = engine_sets(cores[rank], cores[role["m"]], cores[role["a"]], topo)
+    steps = []
+    for step in PLAN["remote"]:
+        ways = []
+        for way in step.split()[1:]:
+            item, rest = way.split(">")
+            dst, eng = rest.split(":")
+            ways.append((role[item[0]], tiles_of(item), role[dst], sets[eng]))
+        steps.append((step[0], ways))
+    return steps
+
+
 def rank_program(g, core, T, topo):
     r = T.rank_of(core)
     if r is None:
         return
     cores = T.cores
-    chips = sorted(set(topo.chip(c) for c in cores))
-    here = chips.index(topo.chip(core))
-    same, other = {}, {}
-    for s, c in enumerate(cores):
-        (same if topo.die(c) == topo.die(core) else other)[chips.index(topo.chip(c))] = s
-    role = {"own": r, "mate": other[here]}
-    made = {"own": 0}
-    for k, v in enumerate(PLAN["lists"]):
-        role["l%d" % k], role["m%d" % k] = same[here ^ v], other[here ^ v]
-        made["l%d" % k] = k + 1
-    for k, v in enumerate(PLAN["codes"]):
-        role["c%d" % k], role["d%d" % k] = same[here ^ v], other[here ^ v]
-    far = cores[same[here ^ 1]]
-    sets = {"on": topo.engines(core, cores[role["mate"]]), "off": topo.engines(core, far)}
-    sets["rest"] = [e for e in sets["on"] if e not in sets["off"]]
-    off = sets["off"]
-    sent = [0]
+    role = roles(r, cores, topo)
+    slot = {}
+    for op in PLAN["vector"]:
+        if op[0] == "a" and role[op[2]] not in slot:
+            slot[role[op[2]]] = len(slot)
 
-    def transfer(dst, engines, sem, src, to):
-        rid, pid = topo.addr(cores[dst])[:2]
-        sent[0] += len(engines)
-        return RemoteDMATransfer(dst_ids=[DstId(rid=rid, pnc=pid)], dma_engine_mask=bits(engines),
-                                 remote_sem=T.sem[sem], src=src, dst=to)
+    ready, lists = {}, {}
+    for op in PLAN["vector"]:
+        if op[0] == "a":
+            item = op.split()[1]
+            s, tt = role[item[0]], tiles_of(item)
+            for o in tt:
+                ready[s, o] = ("s_q%d" % (s * O + tt[0]), 1)
+    for src in range(N):
+        for kind, ways in remote_steps(src, cores, topo):
+            for s, tt, dst, eng in ways:
+                if dst == r and kind == "L":
+                    lists[s] = ("s_al%d" % s, len(eng))
+                elif dst == r:
+                    for o in tt:
+                        ready[s, o] = ("s_ar%d" % (s * O + tt[0]), 2 * len(eng))
 
-    def send(s, ways):
-        q, z = T["w%d" % s], T["z%d" % s]
-        g.remote_dma_fused([transfer(d, e, "s_ar%d" % s, q[:, 0:P].bitcast(dt.uint8), q[:, 0:P].bitcast(dt.uint8))
-                            for d, e in ways], local_sem=T.sem.s_sent)
-        g.remote_dma_fused([transfer(d, e, "s_ar%d" % s, z[:, 0:P], z[:, 0:P]) for d, e in ways], local_sem=T.sem.s_sent)
+    seen = set()
 
-    ways, half = [], len(off) // 2
-    for k in range(len(PLAN["codes"])):
-        ways += [[(role["c%d" % k], off[:half]), (role["d%d" % k], off[half:])]]
-    arrive = {"mate": len(sets[PLAN["mate_eng"]["own"]])}
-    for k in range(len(PLAN["lists"])):
-        arrive["m%d" % k] = len(sets[PLAN["mate_eng"]["l%d" % k]])
-    for k in range(len(PLAN["codes"])):
-        arrive["c%d" % k] = arrive["d%d" % k] = half
+    def once(name, q, sem, val):
+        if (name, sem) not in seen:
+            seen.add((name, sem))
+            q.wait_ge(T.sem[sem], val)
 
     g.sync.dma_start(T.cwl[:, :, :, :], T.cw[:, :]).then_inc(T.sem.s_cw, 16)
     g.sync.dma_start(T.bk1[:, :], T.book[:, 4 * K:8 * K]).then_inc(T.sem.s_b1, 16)
     g.sync.dma_start(T.bk0[:, :], T.book[:, 0:4 * K]).then_inc(T.sem.s_b0, 16)
     g.sync.dma_start(T.xb[:, :], T.x[:, :]).then_inc(T.sem.s_x, 16)
 
-    n = P // 16
     g.vector.wait_ge(T.sem.s_cw, 16)
-    own = T["li%d" % r]
     for m in (1, 0):
         for t in range(4):
-            k = (m * 4 + t) * n
-            g.vector.tensor_scalar(own[:, k:k + n], T.cwl[:, :, m, :], 4.0, float(t), AluOpType.mult,
-                                   AluOpType.add).then_inc(T.sem.s_list, 1)
+            k = (m * 4 + t) * O * LC
+            g.vector.tensor_scalar(T["li%d" % r][:, k:k + O * LC], T.cwl[:, :, m, :], 4.0, float(t), AluOpType.mult,
+                                   AluOpType.add).then_inc(T.sem["s_l%d" % m], 1)
 
-    nl = len(PLAN["lists"])
-    g.wait_ge(T.sem.s_list, 8)
-    for k in range(nl):
-        g.remote_dma_fused([transfer(role["l%d" % k], off, "s_al%d" % r, own[:, :], own[:, :])], local_sem=T.sem.s_sent)
-    g.wait_ge(T.sem.s_q0, 1)
-    first = [(role["mate"], sets[PLAN["mate_eng"]["own"]])]
-    if PLAN["mate_eng"]["own"] == "rest":
-        send(r, first + (ways[0] if ways else []))
-        rem = ways[1:]
-    else:
-        send(r, first)
-        rem = ways
-    for w in rem:
-        send(r, w)
-    for k in range(nl):
-        g.wait_ge(T.sem["s_q%d" % (k + 1)], 1)
-        send(role["l%d" % k], [(role["mate"], sets[PLAN["mate_eng"]["l%d" % k]])])
+    sent = [0]
+
+    def transfer(dst, engines, sem, view):
+        rid, pid = topo.addr(cores[dst])[:2]
+        sent[0] += len(engines)
+        return RemoteDMATransfer(dst_ids=[DstId(rid=rid, pnc=pid)], dma_engine_mask=bits(engines),
+                                 remote_sem=T.sem[sem], src=view, dst=view)
+
+    for kind, ways in remote_steps(r, cores, topo):
+        if kind == "L":
+            once("g", g, "s_l0", 4)
+            once("g", g, "s_l1", 4)
+            g.remote_dma_fused([transfer(d, e, "s_al%d" % s, T["li%d" % s][:, :]) for s, tt, d, e in ways],
+                               local_sem=T.sem.s_sent)
+            continue
+        for s, tt, d, e in ways:
+            for o in tt:
+                once("g", g, *ready[s, o])
+        cut = [("s_ar%d" % (s * O + tt[0]), s, tt[0] * W, (tt[-1] + 1) * W, d, e) for s, tt, d, e in ways]
+        g.remote_dma_fused([transfer(d, e, sem, T["w%d" % s][:, a:b].bitcast(dt.uint8)) for sem, s, a, b, d, e in cut],
+                           local_sem=T.sem.s_sent)
+        g.remote_dma_fused([transfer(d, e, sem, T["z%d" % s][:, a:b]) for sem, s, a, b, d, e in cut],
+                           local_sem=T.sem.s_sent)
     g.wait_ge(T.sem.s_sent, sent[0])
 
-    seen = {"scalar": set(), "vector": set()}
+    order = [(role[w[0]], int(w[1])) for w in PLAN["tensor"].split()]
+    gathered = {}
+    for op in PLAN["scalar"] + PLAN["vector"]:
+        if op[0] == "g":
+            _, item, ts = op.split()
+            s, tt = role[item[0]], tiles_of(item)
+            for t in map(int, ts):
+                for o in tt:
+                    gathered[s, o, t] = "s_g%d%d%d" % (slot[s], tt[0], int(ts[0]) if len(tt) == O else t)
 
-    def once(name, q, sem, val):
-        if sem not in seen[name]:
-            seen[name].add(sem)
-            q.wait_ge(T.sem[sem], val)
+    def list_wait(name, q, s, m):
+        once(name, q, *(("s_l%d" % m, 4) if s == r else lists[s]))
 
-    def list_wait(name, q, who):
-        if who == "own":
-            once(name, q, "s_list", 8)
-        else:
-            once(name, q, "s_al%d" % role[who], len(off))
+    def copy(q, to, src):
+        return q.activation(to, src, ActivationFunctionType.Copy) if q is g.scalar else q.tensor_copy(to, src)
 
-    def evac(q, who, o):
-        i = role[who] * O + o
-        p = PLAN["tensor"].index(who) * O + o
-        q.wait_ge(T.sem["s_mm%d" % i], 1)
-        src, to = T["ps%d" % (p % BANKS)][:, 0:T_COLS], T.yb[:, i * T_COLS:(i + 1) * T_COLS]
-        if q is g.scalar:
-            c = q.activation(to, src, ActivationFunctionType.Copy)
-        else:
-            c = q.tensor_copy(to, src)
-        c.then_inc(T.sem["s_ev%d" % i], 1)
+    for name, q in (("scalar", g.scalar), ("vector", g.vector)):
+        for op in PLAN[name]:
+            op = op.split()
+            if op[0] == "x":
+                q.wait_ge(T.sem.s_x, 16)
+                q.quantize_mx(T.xq[:, 0:T_COLS], T.xz[:, 0:T_COLS], T.xb[:, 0:4 * T_COLS]).then_inc(T.sem.s_xq, 1)
+                continue
+            s, tt = role[op[1][0]], tiles_of(op[1])
+            if op[0] == "e":
+                i = s * O + tt[0]
+                q.wait_ge(T.sem["s_mm%d" % i], 1)
+                copy(q, T.yb[:, i * T_COLS:(i + 1) * T_COLS],
+                     T["ps%d" % (order.index((s, tt[0])) % BANKS)][:, 0:T_COLS]).then_inc(T.sem["s_ev%d" % i], 1)
+                continue
+            ts, li, gb, hb = [int(t) for t in op[2]], T["li%d" % s], T["g%d" % slot[s]], T["h%d" % slot[s]]
+            if op[0] == "g":
+                once(name, q, "s_b1", 16)
+                list_wait(name, q, s, 1)
+                runs = [(ts[0] * O, (ts[-1] + 1) * O)] if len(tt) == O else [(t * O + tt[0], t * O + tt[0] + 1) for t in ts]
+                for a, b in runs:
+                    copy(q, gb[:, a * W:b * W], T.bk1[:, 0:4 * K].indirect(li[:, (4 * O + a) * LC:(4 * O + b) * LC])
+                         ).then_inc(T.sem[gathered[s, tt[0], a // O]], 1)
+                continue
+            once(name, q, "s_b0", 16)
+            list_wait(name, q, s, 0)
+            hs = "s_h%d%d" % (slot[s], tt[0])
+            lo, hi = tt[0], tt[-1] + 1
+            for t in ts:
+                for o in tt:
+                    once(name, q, gathered[s, o, t], 1)
+                a, b = t * O + lo, t * O + hi
+                q.tensor_tensor(hb[:, 4 * W * lo + t:4 * W * hi:4], T.bk0[:, 0:4 * K].indirect(li[:, a * LC:b * LC]),
+                                gb[:, a * W:b * W], AluOpType.add).then_inc(T.sem[hs], 1)
+            q.wait_ge(T.sem[hs], 4)
+            q.quantize_mx(T["w%d" % s][:, lo * W:hi * W], T["z%d" % s][:, lo * W:hi * W],
+                          hb[:, 4 * W * lo:4 * W * hi]).then_inc(T.sem[ready[s, lo][0]], 1)
 
-    for op in PLAN["scalar"]:
-        op = op.split()
-        if op[0] == "e":
-            evac(g.scalar, op[1], int(op[2]))
-            continue
-        i, off16 = made[op[1]], T["li%d" % role[op[1]]]
-        once("scalar", g.scalar, "s_b1", 16)
-        list_wait("scalar", g.scalar, op[1])
-        for t in range(4):
-            k = (4 + t) * n
-            g.scalar.activation(T["g%d" % i][:, t:4 * P:4], T.bk1[:, 0:4 * K].indirect(off16[:, k:k + n]),
-                                ActivationFunctionType.Copy).then_inc(T.sem["s_g%d%d" % (i, t)], 1)
-
-    for op in PLAN["vector"]:
-        op = op.split()
-        if op[0] == "e":
-            evac(g.vector, op[1], int(op[2]))
-        elif op[0] == "x":
-            g.vector.wait_ge(T.sem.s_x, 16)
-            g.vector.quantize_mx(T.xq[:, 0:T_COLS], T.xz[:, 0:T_COLS], T.xb[:, 0:4 * T_COLS]).then_inc(T.sem.s_xq, 1)
-        else:
-            i, s = made[op[1]], role[op[1]]
-            once("vector", g.vector, "s_b0", 16)
-            list_wait("vector", g.vector, op[1])
-            for t in range(4):
-                k = t * n
-                g.vector.wait_ge(T.sem["s_g%d%d" % (i, t)], 1)
-                g.vector.tensor_tensor(T["h%d" % i][:, t:4 * P:4], T.bk0[:, 0:4 * K].indirect(T["li%d" % s][:, k:k + n]),
-                                       T["g%d" % i][:, t:4 * P:4], AluOpType.add).then_inc(T.sem["s_h%d" % i], 1)
-            g.vector.wait_ge(T.sem["s_h%d" % i], 4)
-            g.vector.quantize_mx(T["w%d" % s][:, 0:P], T["z%d" % s][:, 0:P],
-                                 T["h%d" % i][:, 0:4 * P]).then_inc(T.sem["s_q%d" % i], 1)
-
-    order = [(w, o) for w in PLAN["tensor"] for o in range(O)]
     g.tensor.wait_ge(T.sem.s_xq, 1)
-    for p, (who, o) in enumerate(order):
-        s = role[who]
-        if o == 0:
-            if who in made:
-                g.tensor.wait_ge(T.sem["s_q%d" % made[who]], 1)
-            else:
-                g.tensor.wait_ge(T.sem["s_ar%d" % s], 2 * arrive[who])
+    for p, (s, o) in enumerate(order):
+        once("tensor", g.tensor, *ready[s, o])
         if p >= BANKS:
-            pw, po = order[p - BANKS]
-            g.tensor.wait_ge(T.sem["s_ev%d" % (role[pw] * O + po)], 1)
+            g.tensor.wait_ge(T.sem["s_ev%d" % (order[p - BANKS][0] * O + order[p - BANKS][1])], 1)
         g.tensor.matmul_mx(T["ps%d" % (p % BANKS)][:, 0:T_COLS], T["w%d" % s][:, o * W:(o + 1) * W],
                            T["z%d" % s][:, o * W:(o + 1) * W], T.xq[:, 0:T_COLS], T.xz[:, 0:T_COLS],
                            True, True).then_inc(T.sem["s_mm%d" % (s * O + o)], 1)
 
     for group in PLAN["store"]:
-        ss = sorted(role[w] for w in group)
-        for s in ss:
-            for o in range(O):
-                g.sync.wait_ge(T.sem["s_ev%d" % (s * O + o)], 1)
-        a, b = ss[0] * O * T_COLS, (ss[-1] + 1) * O * T_COLS
+        blocks = sorted(role[w[0]] * O + o for w in group.split() for o in tiles_of(w))
+        for i in blocks:
+            g.sync.wait_ge(T.sem["s_ev%d" % i], 1)
+        a, b = blocks[0] * T_COLS, (blocks[-1] + 1) * T_COLS
         g.sync.dma_start(T.y[:, a:b], T.yb[:, a:b]).then_inc(T.sem.s_out, 16)
     g.sync.wait_ge(T.sem.s_out, 16 * len(PLAN["store"]))

@@ -5,11 +5,12 @@ N, O, T_COLS, K = 8, 2, 256, 256
 W = 128
 P = O * W
 BANKS = 8
+ALL_CORES = 64
 LC = W // 16
-SLOTS = 4
+SLOTS = 8
 
 SCRATCH = {
-    "cwl": ("sbuf", [128, O, 2, LC], "int32"),
+    "cwl": ("sbuf", [128, 2 * O, LC], "int32"),
     "bk0": ("sbuf", [128, 4 * K], "bfloat16"),
     "bk1": ("sbuf", [128, 4 * K], "bfloat16"),
     "xb": ("sbuf", [128, 4 * T_COLS], "bfloat16"),
@@ -20,27 +21,29 @@ SCRATCH = {
 for _k in range(N):
     SCRATCH["w%d" % _k] = ("sbuf", [128, P], "float8_e4m3fn_x4")
     SCRATCH["z%d" % _k] = ("sbuf", [128, P], "uint8")
-    SCRATCH["li%d" % _k] = ("sbuf", [128, 8 * O * LC], "uint16")
+    SCRATCH["li%d" % _k] = ("sbuf", [128, 2 * O, 4 * LC], "uint16")
 for _k in range(SLOTS):
-    SCRATCH["g%d" % _k] = ("sbuf", [128, 4 * P], "bfloat16")
-    SCRATCH["h%d" % _k] = ("sbuf", [128, 4 * P], "bfloat16")
+    SCRATCH["g%d" % _k] = ("sbuf", [128, 4 * W], "bfloat16")
+    SCRATCH["h%d" % _k] = ("sbuf", [128, 4 * W], "bfloat16")
 for _k in range(BANKS):
     SCRATCH["ps%d" % _k] = ("psum", [128, 512], "float32")
 
-SEMAPHORES = ["s_cw", "s_b0", "s_b1", "s_x", "s_l0", "s_l1", "s_xq", "s_sent", "s_out"]
-SEMAPHORES += ["s_g%d%d%d" % (i, o, t) for i in range(SLOTS) for o in range(O) for t in range(4)]
-SEMAPHORES += ["s_h%d%d" % (i, o) for i in range(SLOTS) for o in range(O)]
-SEMAPHORES += ["s_al%d" % s for s in range(N)]
-SEMAPHORES += ["s_%s%d" % (k, i) for k in ("q", "ar", "mm", "ev") for i in range(N * O)]
+SEMAPHORES = ["s_cw", "s_bk0", "s_bk1", "s_xb", "s_li", "s_xq", "s_sent", "s_out"]
+SEMAPHORES += ["s_g%d%d" % (i, t) for i in range(SLOTS) for t in range(4)]
+SEMAPHORES += ["s_h%d" % i for i in range(SLOTS)] + ["s_al%d" % s for s in range(N)]
+SEMAPHORES += ["s_%s%d" % (k, i) for k in ("q", "ac", "az", "mm", "ev") for i in range(N * O)]
 
 PLAN = {
-    "remote": ["L o>b:off", "L o>c:off", "S o0>m:rest o0>a:off", "S o1>m:rest o1>a:off", "S b>m:all", "S a>m:all",
-               "S c>m:all"],
-    "tensor": "o0 o1 m0 m1 b0 b1 a0 a1 B0 B1 c0 c1 A0 A1 C0 C1",
-    "scalar": ["g o 01", "g b 01", "e o0", "g b 23", "e o1", "g c 01", "e m0", "g c 23", "e m1", "e b0", "e b1", "e a0",
-               "e a1", "e B0", "e c0", "e A0", "e C0"],
-    "vector": ["g o 23", "a o0 2301", "x", "a o1 0123", "a b 0123", "a c 0123", "e B1", "e c1", "e A1", "e C1"],
-    "store": ["o0", "o1", "m", "b", "a", "B", "c", "A", "C"],
+    "load": ["sync cw", "sync bk1", "sync bk0", "sync xb"],
+    "remote": [["L o1>a:off", "L o1>b+c:off", "S o0>a:off o0>o1:rest", "S o0>b:off", "S o>m:rest", "S a>m:all", "S b>m:all",
+                "S c1>m:all"],
+               ["S o0>c:off", "S o0>C:off"]],
+    "tensor": "o0 o1 a0 a1 m0 m1 b1 b0 A0 A1 c0 c1 B0 B1 C0 C1",
+    "scalar": ["g o0 01", "g o1 0123", "g a1 01", "g a1 23", "g b1 0123", "e o0", "e o1", "g c1 0123", "e a0", "e a1",
+               "e m0", "e m1", "e b1", "e b0", "e A1", "e c1", "e B1", "e C1"],
+    "vector": ["g o0 23", "a o0 2301", "a o1 0123", "x", "a a1 0123", "a b1 0123", "a c1 0123", "e A0", "e c0", "e B0",
+               "e C0"],
+    "store": ["o", "a", "m", "b", "A", "c", "B", "C0", "C1"],
 }
 
 
@@ -57,57 +60,63 @@ def roles(rank, cores, topo):
     return role
 
 
-def engine_sets(core, near, far, topo):
-    on, off = topo.engines(core, near), topo.engines(core, far)
-    rest = [e for e in on if e not in off]
-    h = len(off) // 2
-    return {"all": on, "off": off, "rest": rest, "off0": off[:h], "off1": off[h:], "rest0": rest[:h], "rest1": rest[h:]}
+def crew(rank, cores, topo):
+    c = cores[rank]
+    near = [k for k in topo.cores_of(c) if topo.die(k) == topo.die(c) and topo.addr(k)[2] != topo.addr(c)[2]]
+    return [c] + near + [k for k in range(ALL_CORES) if topo.mates(topo.chip(k), topo.chip(c))
+                         and topo.die(k) == topo.die(c) and topo.may_write(k, c)]
 
 
 def tiles_of(item):
     return [int(item[1])] if len(item) > 1 else list(range(O))
 
 
-def remote_steps(rank, cores, topo):
-    role = roles(rank, cores, topo)
-    sets = engine_sets(cores[rank], cores[role["m"]], cores[role["a"]], topo)
+def remote_steps(rank, who, cores, topo):
+    role, core = roles(rank, cores, topo), crew(rank, cores, topo)[who]
+    on, off = topo.engines(core, min(set(topo.cores_of(core)) - {core})), topo.engines(core, cores[role["a"]])
+    rest, h = [e for e in on if e not in off], len(off) // 2
+    sets = {"all": on, "off": off, "rest": rest, "off0": off[:h], "off1": off[h:], "rest0": rest[:h], "rest1": rest[h:]}
     steps = []
-    for step in PLAN["remote"]:
+    for step in PLAN["remote"][who]:
         ways = []
         for way in step.split()[1:]:
-            item, rest = way.split(">")
-            dst, eng = rest.split(":")
-            ways.append((role[item[0]], tiles_of(item), role[dst], sets[eng]))
-        steps.append((step[0], ways))
+            item, to = way.split(">")
+            dsts, eng = to.split(":")
+            ways.append((role[item[0]], tiles_of(item),
+                         [crew(role[d[0]], cores, topo)[int(d[1:] or 0)] for d in dsts.split("+")], sets[eng]))
+        steps += [(kind, ways) for kind in ("CZ" if step[0] == "S" else step[0])]
     return steps
 
 
 def rank_program(g, core, T, topo):
-    r = T.rank_of(core)
-    if r is None:
-        return
     cores = T.cores
+    place = [(s, who) for s in range(N) for who in range(len(PLAN["remote"])) if crew(s, cores, topo)[who] == core]
+    if not place:
+        return
+    r, who = place[0]
     role = roles(r, cores, topo)
-    slot = {}
-    for op in PLAN["vector"]:
-        if op[0] == "a" and role[op[2]] not in slot:
-            slot[role[op[2]]] = len(slot)
 
-    ready, lists = {}, {}
-    for op in PLAN["vector"]:
-        if op[0] == "a":
-            item = op.split()[1]
-            s, tt = role[item[0]], tiles_of(item)
-            for o in tt:
-                ready[s, o] = ("s_q%d" % (s * O + tt[0]), 1)
+    def tile(word):
+        return role[word[0]], int(word[1])
+
+    ready, slot = {}, {}
+    if who == 0:
+        for o in range(O):
+            ready["L", r, o] = ("s_li", 4)
+        for op in PLAN["vector"]:
+            if op[0] == "a":
+                s, o = tile(op.split()[1])
+                slot[s, o] = len(slot)
+                ready["C", s, o] = ready["Z", s, o] = ("s_q%d" % (s * O + o), 1)
+    arrival = {"L": lambda s, tt: "s_al%d" % s, "C": lambda s, tt: "s_ac%d" % (s * O + tt[0]),
+               "Z": lambda s, tt: "s_az%d" % (s * O + tt[0])}
     for src in range(N):
-        for kind, ways in remote_steps(src, cores, topo):
-            for s, tt, dst, eng in ways:
-                if dst == r and kind == "L":
-                    lists[s] = ("s_al%d" % s, len(eng))
-                elif dst == r:
-                    for o in tt:
-                        ready[s, o] = ("s_ar%d" % (s * O + tt[0]), 2 * len(eng))
+        for member in range(len(PLAN["remote"])):
+            for kind, ways in remote_steps(src, member, cores, topo):
+                for s, tt, dsts, eng in ways:
+                    if core in dsts:
+                        for o in tt:
+                            ready[kind, s, o] = (arrival[kind](s, tt), len(eng))
 
     seen = set()
 
@@ -116,99 +125,87 @@ def rank_program(g, core, T, topo):
             seen.add((name, sem))
             q.wait_ge(T.sem[sem], val)
 
-    g.sync.dma_start(T.cwl[:, :, :, :], T.cw[:, :]).then_inc(T.sem.s_cw, 16)
-    g.sync.dma_start(T.bk1[:, :], T.book[:, 4 * K:8 * K]).then_inc(T.sem.s_b1, 16)
-    g.sync.dma_start(T.bk0[:, :], T.book[:, 0:4 * K]).then_inc(T.sem.s_b0, 16)
-    g.sync.dma_start(T.xb[:, :], T.x[:, :]).then_inc(T.sem.s_x, 16)
+    def view(kind, s, tt):
+        a, b = tt[0], tt[-1] + 1
+        if kind == "L":
+            return T["li%d" % s][:, 2 * a:2 * b, :]
+        return T["w%d" % s][:, a * W:b * W].bitcast(dt.uint8) if kind == "C" else T["z%d" % s][:, a * W:b * W]
+
+    sent = 0
+    for kind, ways in remote_steps(r, who, cores, topo):
+        transfers = []
+        for s, tt, dsts, eng in ways:
+            for o in tt:
+                once("g", g, *ready[kind, s, o])
+            transfers.append(RemoteDMATransfer(
+                dst_ids=[DstId(rid=topo.addr(d)[0], pnc=topo.addr(d)[1]) for d in dsts], dma_engine_mask=bits(eng),
+                remote_sem=T.sem[arrival[kind](s, tt)], srcs=[view(kind, s, tt)], dsts=[view(kind, s, tt) for d in dsts]))
+            sent += len(eng)
+        g.remote_dma_fused(transfers, local_sem=T.sem.s_sent)
+    if sent:
+        g.wait_ge(T.sem.s_sent, sent)
+    if who:
+        return
+
+    queue = {"sync": g.sync, "scalar": g.scalar, "vector": g.vector}
+    loads = {"cw": (T.cwl[:, :, :], T.cw[:, :]), "bk0": (T.bk0[:, :], T.book[:, 0:4 * K]),
+             "bk1": (T.bk1[:, :], T.book[:, 4 * K:8 * K]), "xb": (T.xb[:, :], T.x[:, :])}
+    for op in PLAN["load"]:
+        name, what = op.split()
+        queue[name].dma_start(*loads[what]).then_inc(T.sem["s_" + what], 16)
 
     g.vector.wait_ge(T.sem.s_cw, 16)
-    for m in (1, 0):
-        for t in range(4):
-            k = (m * 4 + t) * O * LC
-            g.vector.tensor_scalar(T["li%d" % r][:, k:k + O * LC], T.cwl[:, :, m, :], 4.0, float(t), AluOpType.mult,
-                                   AluOpType.add).then_inc(T.sem["s_l%d" % m], 1)
+    for t in range(4):
+        g.vector.tensor_scalar(T["li%d" % r][:, :, t * LC:(t + 1) * LC], T.cwl[:, :, :], 4.0, float(t), AluOpType.mult,
+                               AluOpType.add).then_inc(T.sem.s_li, 1)
 
-    sent = [0]
-
-    def transfer(dst, engines, sem, view):
-        rid, pid = topo.addr(cores[dst])[:2]
-        sent[0] += len(engines)
-        return RemoteDMATransfer(dst_ids=[DstId(rid=rid, pnc=pid)], dma_engine_mask=bits(engines),
-                                 remote_sem=T.sem[sem], src=view, dst=view)
-
-    for kind, ways in remote_steps(r, cores, topo):
-        if kind == "L":
-            once("g", g, "s_l0", 4)
-            once("g", g, "s_l1", 4)
-            g.remote_dma_fused([transfer(d, e, "s_al%d" % s, T["li%d" % s][:, :]) for s, tt, d, e in ways],
-                               local_sem=T.sem.s_sent)
-            continue
-        for s, tt, d, e in ways:
-            for o in tt:
-                once("g", g, *ready[s, o])
-        cut = [("s_ar%d" % (s * O + tt[0]), s, tt[0] * W, (tt[-1] + 1) * W, d, e) for s, tt, d, e in ways]
-        g.remote_dma_fused([transfer(d, e, sem, T["w%d" % s][:, a:b].bitcast(dt.uint8)) for sem, s, a, b, d, e in cut],
-                           local_sem=T.sem.s_sent)
-        g.remote_dma_fused([transfer(d, e, sem, T["z%d" % s][:, a:b]) for sem, s, a, b, d, e in cut],
-                           local_sem=T.sem.s_sent)
-    g.wait_ge(T.sem.s_sent, sent[0])
-
-    order = [(role[w[0]], int(w[1])) for w in PLAN["tensor"].split()]
+    order = [tile(w) for w in PLAN["tensor"].split()]
     gathered = {}
     for op in PLAN["scalar"] + PLAN["vector"]:
         if op[0] == "g":
             _, item, ts = op.split()
-            s, tt = role[item[0]], tiles_of(item)
-            for t in map(int, ts):
-                for o in tt:
-                    gathered[s, o, t] = "s_g%d%d%d" % (slot[s], tt[0], int(ts[0]) if len(tt) == O else t)
-
-    def list_wait(name, q, s, m):
-        once(name, q, *(("s_l%d" % m, 4) if s == r else lists[s]))
+            for t in ts:
+                gathered[tile(item), int(t)] = "s_g%d%s" % (slot[tile(item)], ts[0])
 
     def copy(q, to, src):
         return q.activation(to, src, ActivationFunctionType.Copy) if q is g.scalar else q.tensor_copy(to, src)
 
-    for name, q in (("scalar", g.scalar), ("vector", g.vector)):
+    for name in ("scalar", "vector"):
+        q = queue[name]
         for op in PLAN[name]:
             op = op.split()
             if op[0] == "x":
-                q.wait_ge(T.sem.s_x, 16)
+                q.wait_ge(T.sem.s_xb, 16)
                 q.quantize_mx(T.xq[:, 0:T_COLS], T.xz[:, 0:T_COLS], T.xb[:, 0:4 * T_COLS]).then_inc(T.sem.s_xq, 1)
                 continue
-            s, tt = role[op[1][0]], tiles_of(op[1])
+            s, o = tile(op[1])
             if op[0] == "e":
-                i = s * O + tt[0]
+                i = s * O + o
                 q.wait_ge(T.sem["s_mm%d" % i], 1)
                 copy(q, T.yb[:, i * T_COLS:(i + 1) * T_COLS],
-                     T["ps%d" % (order.index((s, tt[0])) % BANKS)][:, 0:T_COLS]).then_inc(T.sem["s_ev%d" % i], 1)
+                     T["ps%d" % (order.index((s, o)) % BANKS)][:, 0:T_COLS]).then_inc(T.sem["s_ev%d" % i], 1)
                 continue
-            ts, li, gb, hb = [int(t) for t in op[2]], T["li%d" % s], T["g%d" % slot[s]], T["h%d" % slot[s]]
+            ts, li, gb, hb = [int(t) for t in op[2]], T["li%d" % s], T["g%d" % slot[s, o]], T["h%d" % slot[s, o]]
+            once(name, q, "s_bk1" if op[0] == "g" else "s_bk0", 16)
+            once(name, q, *ready["L", s, o])
             if op[0] == "g":
-                once(name, q, "s_b1", 16)
-                list_wait(name, q, s, 1)
-                runs = [(ts[0] * O, (ts[-1] + 1) * O)] if len(tt) == O else [(t * O + tt[0], t * O + tt[0] + 1) for t in ts]
-                for a, b in runs:
-                    copy(q, gb[:, a * W:b * W], T.bk1[:, 0:4 * K].indirect(li[:, (4 * O + a) * LC:(4 * O + b) * LC])
-                         ).then_inc(T.sem[gathered[s, tt[0], a // O]], 1)
+                a, b = ts[0], ts[-1] + 1
+                copy(q, gb[:, a * W:b * W], T.bk1[:, 0:4 * K].indirect(li[:, 2 * o + 1, a * LC:b * LC])
+                     ).then_inc(T.sem[gathered[(s, o), a]], 1)
                 continue
-            once(name, q, "s_b0", 16)
-            list_wait(name, q, s, 0)
-            hs = "s_h%d%d" % (slot[s], tt[0])
-            lo, hi = tt[0], tt[-1] + 1
+            hs = T.sem["s_h%d" % slot[s, o]]
             for t in ts:
-                for o in tt:
-                    once(name, q, gathered[s, o, t], 1)
-                a, b = t * O + lo, t * O + hi
-                q.tensor_tensor(hb[:, 4 * W * lo + t:4 * W * hi:4], T.bk0[:, 0:4 * K].indirect(li[:, a * LC:b * LC]),
-                                gb[:, a * W:b * W], AluOpType.add).then_inc(T.sem[hs], 1)
-            q.wait_ge(T.sem[hs], 4)
-            q.quantize_mx(T["w%d" % s][:, lo * W:hi * W], T["z%d" % s][:, lo * W:hi * W],
-                          hb[:, 4 * W * lo:4 * W * hi]).then_inc(T.sem[ready[s, lo][0]], 1)
+                once(name, q, gathered[(s, o), t], 1)
+                q.tensor_tensor(hb[:, t:4 * W:4], T.bk0[:, 0:4 * K].indirect(li[:, 2 * o, t * LC:(t + 1) * LC]),
+                                gb[:, t * W:(t + 1) * W], AluOpType.add).then_inc(hs, 1)
+            q.wait_ge(hs, 4)
+            q.quantize_mx(T["w%d" % s][:, o * W:(o + 1) * W], T["z%d" % s][:, o * W:(o + 1) * W],
+                          hb[:, 0:4 * W]).then_inc(T.sem[ready["C", s, o][0]], 1)
 
     g.tensor.wait_ge(T.sem.s_xq, 1)
     for p, (s, o) in enumerate(order):
-        once("tensor", g.tensor, *ready[s, o])
+        once("tensor", g.tensor, *ready["C", s, o])
+        once("tensor", g.tensor, *ready["Z", s, o])
         if p >= BANKS:
             g.tensor.wait_ge(T.sem["s_ev%d" % (order[p - BANKS][0] * O + order[p - BANKS][1])], 1)
         g.tensor.matmul_mx(T["ps%d" % (p % BANKS)][:, 0:T_COLS], T["w%d" % s][:, o * W:(o + 1) * W],

@@ -3,14 +3,16 @@ from concourse.mybir import dt, AluOpType, ActivationFunctionType
 
 N, O, T_COLS, K = 8, 2, 256, 256
 W = 128
+H = W // 2
 P = O * W
 BANKS = 8
 ALL_CORES = 64
 LC = W // 16
-SLOTS = 8
+SLOTS = 6
 
 SCRATCH = {
     "cwl": ("sbuf", [128, 2 * O, LC], "int32"),
+    "raw": ("sbuf", [128, 2, LC], "int32"),
     "bk0": ("sbuf", [128, 4 * K], "bfloat16"),
     "bk1": ("sbuf", [128, 4 * K], "bfloat16"),
     "xb": ("sbuf", [128, 4 * T_COLS], "bfloat16"),
@@ -28,21 +30,24 @@ for _k in range(SLOTS):
 for _k in range(BANKS):
     SCRATCH["ps%d" % _k] = ("psum", [128, 512], "float32")
 
-SEMAPHORES = ["s_cw", "s_bk0", "s_bk1", "s_xb", "s_li", "s_xq", "s_sent", "s_out"]
-SEMAPHORES += ["s_g%d%d" % (i, t) for i in range(SLOTS) for t in range(4)]
+SEMAPHORES = ["s_cw", "s_bk0", "s_bk1", "s_xb", "s_li", "s_lr", "s_xq", "s_sent", "s_out", "s_raw"]
+SEMAPHORES += ["s_mix%s%d" % (k, h) for k in "cz" for h in range(2)]
+SEMAPHORES += ["s_g%d%d" % (i, t) for i in range(SLOTS) for t in range(4)] + ["s_ew%d" % i for i in range(N * O)]
 SEMAPHORES += ["s_h%d" % i for i in range(SLOTS)] + ["s_al%d" % s for s in range(N)]
-SEMAPHORES += ["s_%s%d" % (k, i) for k in ("q", "ac", "az", "mm", "ev") for i in range(N * O)]
+SEMAPHORES += ["s_%s%d" % (k, i) for k in ("ac", "az", "mm", "mw", "ev") for i in range(N * O)]
 
 PLAN = {
-    "load": ["sync cw", "sync bk1", "sync bk0", "sync xb"],
-    "remote": [["L o1>a:off", "L o1>b+c:off", "S o0>a:off o0>o1:rest", "S o0>b:off", "S o>m:rest", "S a>m:all", "S b>m:all",
-                "S c1>m:all"],
+    "names": ["oabc", "oabc"],
+    "halved": "C1",
+    "load": ["sync cw", "scalar bk1", "sync bk0", "sync xb"],
+    "remote": [["W o1>c:off", "L o1>a:off", "L o1>b:off", "S o0>a:off o0>o1:rest", "S o0>b:off o0>m:rest", "S o1>m:rest",
+                "S a0>m:rest", "S a1>m:all", "S b0>m:all", "S b1>m:all", "S c1>m:all"],
                ["S o0>c:off", "S o0>C:off"]],
     "tensor": "o0 o1 a0 a1 m0 m1 b1 b0 A0 A1 c0 c1 B0 B1 C0 C1",
-    "scalar": ["g o0 01", "g o1 0123", "g a1 01", "g a1 23", "g b1 0123", "e o0", "e o1", "g c1 0123", "e a0", "e a1",
-               "e m0", "e m1", "e b1", "e b0", "e A1", "e c1", "e B1", "e C1"],
-    "vector": ["g o0 23", "a o0 2301", "a o1 0123", "x", "a a1 0123", "a b1 0123", "a c1 0123", "e A0", "e c0", "e B0",
-               "e C0"],
+    "scalar": ["g o0 0", "g o0 12", "g o1 0123", "g a1 01", "g a1 23", "g b1 0123", "e o0", "e o1", "g c1 0123", "e a0",
+               "e a1", "e m0", "e m1", "e b1", "e b0", "e A1", "e c1", "e B1", "e C1 1"],
+    "vector": ["g o0 3", "a o0 0312", "x 0", "q o0", "a o1 0123", "x 1", "q o1", "r c 01", "a a1 0123", "r c 23", "q a1",
+               "a b1 0123", "a c1 0", "q b1", "a c1 123", "q c1", "e A0", "e c0", "e B0", "e C0", "e C1 0"],
     "store": ["o", "a", "m", "b", "A", "c", "B", "C0", "C1"],
 }
 
@@ -56,7 +61,8 @@ def roles(rank, cores, topo):
     here, die = chips.index(topo.chip(cores[rank])), topo.die(cores[rank])
     role = {}
     for s, c in enumerate(cores):
-        role[("oabc" if topo.die(c) == die else "mABC")[chips.index(topo.chip(c)) ^ here]] = s
+        names = PLAN["names"][topo.die(c)]
+        role[(names if topo.die(c) == die else "m" + names[1:].upper())[chips.index(topo.chip(c)) ^ here]] = s
     return role
 
 
@@ -68,7 +74,7 @@ def crew(rank, cores, topo):
 
 
 def tiles_of(item):
-    return [int(item[1])] if len(item) > 1 else list(range(O))
+    return [item[1] if item[1] in "hpq" else int(item[1])] if len(item) > 1 else list(range(O))
 
 
 def remote_steps(rank, who, cores, topo):
@@ -82,9 +88,8 @@ def remote_steps(rank, who, cores, topo):
         for way in step.split()[1:]:
             item, to = way.split(">")
             dsts, eng = to.split(":")
-            ways.append((role[item[0]], tiles_of(item),
-                         [crew(role[d[0]], cores, topo)[int(d[1:] or 0)] for d in dsts.split("+")], sets[eng]))
-        steps += [(kind, ways) for kind in ("CZ" if step[0] == "S" else step[0])]
+            ways.append((role[item[0]], tiles_of(item), [(role[d[0]], int(d[1:] or 0)) for d in dsts.split("+")], sets[eng]))
+        steps += [(kind, ways) for kind in {"S": "CZ", "R": "ZC"}.get(step[0], step[0])]
     return steps
 
 
@@ -95,28 +100,54 @@ def rank_program(g, core, T, topo):
         return
     r, who = place[0]
     role = roles(r, cores, topo)
+    mixed = any("oh>" in step for step in PLAN["remote"][0])
+    made_mix, come_mix = (role["c"], 1), (role["C"], 1)
 
     def tile(word):
         return role[word[0]], int(word[1])
 
+    def kept(s):
+        return topo.die(cores[s])
+
+    def landing(s, tt, d):
+        if tt == ["h"]:
+            a = W + (1 - kept(s)) * H
+            return (s if d[0] == s else roles(d[0], cores, topo)["C"]), a, a + H
+        return s, tt[0] * W, (tt[-1] + 1) * W
+
+    def arrival(kind, s, tt, d):
+        if tt[0] in ("p", "q"):
+            return "s_raw"
+        k, a, _ = landing(s, tt, d)
+        if tt == ["h"]:
+            return "s_mix%s%d" % (kind.lower(), kept(s))
+        return "s_al%d" % s if kind in "LW" else "s_a%s%d" % (kind.lower(), k * O + a // W)
+
     ready, slot = {}, {}
     if who == 0:
         for o in range(O):
-            ready["L", r, o] = ("s_li", 4)
+            ready["L", r, o], ready["W", r, o] = ("s_li", 4), ("s_cw", 16)
         for op in PLAN["vector"]:
-            if op[0] == "a":
+            if op[0] == "r":
+                ready["L", role[op.split()[1]], 1] = ("s_lr", 4)
+            if op[0] == "q":
                 s, o = tile(op.split()[1])
                 slot[s, o] = len(slot)
-                ready["C", s, o] = ready["Z", s, o] = ("s_q%d" % (s * O + o), 1)
-    arrival = {"L": lambda s, tt: "s_al%d" % s, "C": lambda s, tt: "s_ac%d" % (s * O + tt[0]),
-               "Z": lambda s, tt: "s_az%d" % (s * O + tt[0])}
+                ready["C", s, o] = ready["Z", s, o] = ("s_ac%d" % (s * O + o), 1)
+        ready["C", r, "h"] = ready["Z", r, "h"] = ready["C", r, 1]
+        ready["W", r, "p"] = ready["W", r, "q"] = ready["W", r, 1]
+    count = {}
     for src in range(N):
         for member in range(len(PLAN["remote"])):
             for kind, ways in remote_steps(src, member, cores, topo):
                 for s, tt, dsts, eng in ways:
-                    if core in dsts:
+                    if (r, who) in dsts:
+                        sem = arrival(kind, s, tt, (r, who))
+                        count[sem] = count.get(sem, 0) + len(eng)
                         for o in tt:
-                            ready[kind, s, o] = (arrival[kind](s, tt), len(eng))
+                            ready[kind, s, o] = (sem, count[sem])
+    if mixed and who == 0:
+        ready["W", role["c"], 1] = ("s_raw", count["s_raw"])
 
     seen = set()
 
@@ -125,11 +156,16 @@ def rank_program(g, core, T, topo):
             seen.add((name, sem))
             q.wait_ge(T.sem[sem], val)
 
-    def view(kind, s, tt):
-        a, b = tt[0], tt[-1] + 1
+    def view(kind, s, tt, d):
+        if tt[0] in ("p", "q"):
+            m, a, b = "pq".index(tt[0]), kept(s) * LC // 2, (kept(s) + 1) * LC // 2
+            return T.cwl[:, 2 + m, a:b] if d == (s, 0) else T.raw[:, m, a:b]
+        k, a, b = landing(s, tt, d)
+        if kind == "W":
+            return T.cwl[:, 2:4, :] if d == (s, 0) else T.raw[:, :, :]
         if kind == "L":
-            return T["li%d" % s][:, 2 * a:2 * b, :]
-        return T["w%d" % s][:, a * W:b * W].bitcast(dt.uint8) if kind == "C" else T["z%d" % s][:, a * W:b * W]
+            return T["li%d" % s][:, 2 * tt[0]:2 * tt[-1] + 2, :]
+        return T["w%d" % k][:, a:b].bitcast(dt.uint8) if kind == "C" else T["z%d" % k][:, a:b]
 
     sent = 0
     for kind, ways in remote_steps(r, who, cores, topo):
@@ -137,11 +173,25 @@ def rank_program(g, core, T, topo):
         for s, tt, dsts, eng in ways:
             for o in tt:
                 once("g", g, *ready[kind, s, o])
-            transfers.append(RemoteDMATransfer(
-                dst_ids=[DstId(rid=topo.addr(d)[0], pnc=topo.addr(d)[1]) for d in dsts], dma_engine_mask=bits(eng),
-                remote_sem=T.sem[arrival[kind](s, tt)], srcs=[view(kind, s, tt)], dsts=[view(kind, s, tt) for d in dsts]))
-            sent += len(eng)
-        g.remote_dma_fused(transfers, local_sem=T.sem.s_sent)
+            to = [topo.addr(crew(d, cores, topo)[k]) for d, k in dsts]
+            sems = set(arrival(kind, s, tt, d) for d in dsts)
+            for sem in sorted(sems):
+                part = [i for i, d in enumerate(dsts) if arrival(kind, s, tt, d) == sem]
+                transfers.append([RemoteDMATransfer(
+                    dst_ids=[DstId(rid=to[i][0], pnc=to[i][1]) for i in part], dma_engine_mask=bits(eng),
+                    remote_sem=T.sem[sem], srcs=[view(kind, s, tt, (r, who))],
+                    dsts=[view(kind, s, tt, dsts[i]) for i in part]), bits(eng)])
+                sent += len(eng)
+        while transfers:
+            now, later, taken = [], [], 0
+            for tr, mask in transfers:
+                if mask & taken:
+                    later.append([tr, mask])
+                else:
+                    now.append(tr)
+                    taken |= mask
+            g.remote_dma_fused(now, local_sem=T.sem.s_sent)
+            transfers = later
     if sent:
         g.wait_ge(T.sem.s_sent, sent)
     if who:
@@ -159,7 +209,10 @@ def rank_program(g, core, T, topo):
         g.vector.tensor_scalar(T["li%d" % r][:, :, t * LC:(t + 1) * LC], T.cwl[:, :, :], 4.0, float(t), AluOpType.mult,
                                AluOpType.add).then_inc(T.sem.s_li, 1)
 
-    order = [tile(w) for w in PLAN["tensor"].split()]
+    halved = [tile(w) for w in PLAN["halved"].split()]
+    jobs = []
+    for w in PLAN["tensor"].split():
+        jobs += [tile(w) + (k, k * W, k * W + W) for k in range(2)] if tile(w) in halved else [tile(w) + (0, 0, T_COLS)]
     gathered = {}
     for op in PLAN["scalar"] + PLAN["vector"]:
         if op[0] == "g":
@@ -175,47 +228,75 @@ def rank_program(g, core, T, topo):
         for op in PLAN[name]:
             op = op.split()
             if op[0] == "x":
-                q.wait_ge(T.sem.s_xb, 16)
-                q.quantize_mx(T.xq[:, 0:T_COLS], T.xz[:, 0:T_COLS], T.xb[:, 0:4 * T_COLS]).then_inc(T.sem.s_xq, 1)
+                a, b = (int(op[1]) * W, int(op[1]) * W + W) if op[1:] else (0, T_COLS)
+                once(name, q, "s_xb", 16)
+                q.quantize_mx(T.xq[:, a:b], T.xz[:, a:b], T.xb[:, 4 * a:4 * b]).then_inc(T.sem.s_xq, (b - a) // W)
+                continue
+            if op[0] == "r":
+                s = role[op[1]]
+                once(name, q, *ready["W", s, 1])
+                for t in op[2]:
+                    q.tensor_scalar(T["li%d" % s][:, 2:4, int(t) * LC:(int(t) + 1) * LC], T.raw[:, :, :], 4.0, float(t), AluOpType.mult,
+                                    AluOpType.add).then_inc(T.sem.s_lr, 1)
                 continue
             s, o = tile(op[1])
             if op[0] == "e":
-                i = s * O + o
-                q.wait_ge(T.sem["s_mm%d" % i], 1)
-                copy(q, T.yb[:, i * T_COLS:(i + 1) * T_COLS],
-                     T["ps%d" % (order.index((s, o)) % BANKS)][:, 0:T_COLS]).then_inc(T.sem["s_ev%d" % i], 1)
+                i, part = s * O + o, int(op[2]) if op[2:] else 0
+                p = [k for k, job in enumerate(jobs) if job[:3] == (s, o, part)][0]
+                a, b = jobs[p][3:]
+                q.wait_ge(T.sem["s_%s%d" % ("mw" if part else "mm", i)], 1)
+                copy(q, T.yb[:, i * T_COLS + a:i * T_COLS + b],
+                     T["ps%d" % (p % BANKS)][:, 0:b - a]).then_inc(T.sem["s_%s%d" % ("ew" if part else "ev", i)], 1)
                 continue
-            ts, li, gb, hb = [int(t) for t in op[2]], T["li%d" % s], T["g%d" % slot[s, o]], T["h%d" % slot[s, o]]
+            gb, hb, hs = T["g%d" % slot[s, o]], T["h%d" % slot[s, o]], T.sem["s_h%d" % slot[s, o]]
+            if op[0] == "q":
+                q.wait_ge(hs, 4)
+                q.quantize_mx(T["w%d" % s][:, o * W:(o + 1) * W], T["z%d" % s][:, o * W:(o + 1) * W],
+                              hb[:, 0:4 * W]).then_inc(T.sem[ready["C", s, o][0]], 1)
+                continue
+            ts = [int(t) for t in op[2]]
+            li, at, listed = T["li%d" % s], 2 * o, ready["L", s, o]
             once(name, q, "s_bk1" if op[0] == "g" else "s_bk0", 16)
-            once(name, q, *ready["L", s, o])
+            once(name, q, *listed)
             if op[0] == "g":
                 a, b = ts[0], ts[-1] + 1
-                copy(q, gb[:, a * W:b * W], T.bk1[:, 0:4 * K].indirect(li[:, 2 * o + 1, a * LC:b * LC])
+                copy(q, gb[:, a * W:b * W], T.bk1[:, 0:4 * K].indirect(li[:, at + 1, a * LC:b * LC])
                      ).then_inc(T.sem[gathered[(s, o), a]], 1)
                 continue
-            hs = T.sem["s_h%d" % slot[s, o]]
             for t in ts:
                 once(name, q, gathered[(s, o), t], 1)
-                q.tensor_tensor(hb[:, t:4 * W:4], T.bk0[:, 0:4 * K].indirect(li[:, 2 * o, t * LC:(t + 1) * LC]),
+                q.tensor_tensor(hb[:, t:4 * W:4], T.bk0[:, 0:4 * K].indirect(li[:, at, t * LC:(t + 1) * LC]),
                                 gb[:, t * W:(t + 1) * W], AluOpType.add).then_inc(hs, 1)
-            q.wait_ge(hs, 4)
-            q.quantize_mx(T["w%d" % s][:, o * W:(o + 1) * W], T["z%d" % s][:, o * W:(o + 1) * W],
-                          hb[:, 0:4 * W]).then_inc(T.sem[ready["C", s, o][0]], 1)
 
-    g.tensor.wait_ge(T.sem.s_xq, 1)
-    for p, (s, o) in enumerate(order):
-        once("tensor", g.tensor, *ready["C", s, o])
-        once("tensor", g.tensor, *ready["Z", s, o])
+    g.tensor.wait_ge(T.sem.s_xq, T_COLS // W)
+    for p, (s, o, part, a, b) in enumerate(jobs):
+        for k, piece in ([(role["c"], "h"), (role["C"], "h")] if mixed and (s, o) == come_mix else [(s, o)]):
+            once("tensor", g.tensor, *ready["C", k, piece])
+            once("tensor", g.tensor, *ready["Z", k, piece])
         if p >= BANKS:
-            g.tensor.wait_ge(T.sem["s_ev%d" % (order[p - BANKS][0] * O + order[p - BANKS][1])], 1)
-        g.tensor.matmul_mx(T["ps%d" % (p % BANKS)][:, 0:T_COLS], T["w%d" % s][:, o * W:(o + 1) * W],
-                           T["z%d" % s][:, o * W:(o + 1) * W], T.xq[:, 0:T_COLS], T.xz[:, 0:T_COLS],
-                           True, True).then_inc(T.sem["s_mm%d" % (s * O + o)], 1)
+            s2, o2, part2 = jobs[p - BANKS][:3]
+            g.tensor.wait_ge(T.sem["s_%s%d" % ("ew" if part2 else "ev", s2 * O + o2)], 1)
+        g.tensor.matmul_mx(T["ps%d" % (p % BANKS)][:, 0:b - a], T["w%d" % s][:, o * W:(o + 1) * W],
+                           T["z%d" % s][:, o * W:(o + 1) * W], T.xq[:, a:b], T.xz[:, a:b],
+                           True, True).then_inc(T.sem["s_%s%d" % ("mw" if part else "mm", s * O + o)], 1)
 
+    stores = 0
     for group in PLAN["store"]:
-        blocks = sorted(role[w[0]] * O + o for w in group.split() for o in tiles_of(w))
+        for w in group.split():
+            if w[0] == "@":
+                g.sync.wait_ge(T.sem[ready[("C",) + tile(w[1:])][0]], 1)
+        items = [(role[w[0]], o) for w in group.split() if w[0] != "@" for o in tiles_of(w)]
+        blocks = sorted(s * O + o for s, o in items)
         for i in blocks:
             g.sync.wait_ge(T.sem["s_ev%d" % i], 1)
+            if divmod(i, O) in halved:
+                g.sync.wait_ge(T.sem["s_ew%d" % i], 1)
         a, b = blocks[0] * T_COLS, (blocks[-1] + 1) * T_COLS
-        g.sync.dma_start(T.y[:, a:b], T.yb[:, a:b]).then_inc(T.sem.s_out, 16)
-    g.sync.wait_ge(T.sem.s_out, 16 * len(PLAN["store"]))
+        pieces = [(0, 128, a)]
+        if mixed and items[0] in (made_mix, come_mix):
+            halves = {s: kept(s) if items[0] == made_mix else 1 - kept(s) for s in (role["c"], role["C"])}
+            pieces = [(h * H, (h + 1) * H, (s * O + 1) * T_COLS) for s, h in halves.items()]
+        for p0, p1, to in pieces:
+            g.sync.dma_start(T.y[p0:p1, to:to + b - a], T.yb[p0:p1, a:b]).then_inc(T.sem.s_out, 16)
+            stores += 1
+    g.sync.wait_ge(T.sem.s_out, 16 * stores)

from concourse.bass import DstId, RemoteDMATransfer
from concourse.mybir import dt, AluOpType, ActivationFunctionType

N, O, T_COLS, K = 8, 2, 256, 256
W = 128
H = W // 2
P = O * W
BANKS = 8
ALL_CORES = 64
LC = W // 16
SLOTS = 6

SCRATCH = {
    "cwl": ("sbuf", [128, 2 * O, LC], "int32"),
    "raw": ("sbuf", [128, 2, LC], "int32"),
    "bk0": ("sbuf", [128, 4 * K], "bfloat16"),
    "bk1": ("sbuf", [128, 4 * K], "bfloat16"),
    "xb": ("sbuf", [128, 4 * T_COLS], "bfloat16"),
    "xq": ("sbuf", [128, T_COLS], "float8_e4m3fn_x4"),
    "xz": ("sbuf", [128, T_COLS], "uint8"),
    "yb": ("sbuf", [128, N * O * T_COLS], "float32"),
}
for _k in range(N):
    SCRATCH["w%d" % _k] = ("sbuf", [128, P], "float8_e4m3fn_x4")
    SCRATCH["z%d" % _k] = ("sbuf", [128, P], "uint8")
    SCRATCH["li%d" % _k] = ("sbuf", [128, 2 * O, 4 * LC], "uint16")
for _k in range(SLOTS):
    SCRATCH["g%d" % _k] = ("sbuf", [128, 4 * W], "bfloat16")
    SCRATCH["h%d" % _k] = ("sbuf", [128, 4 * W], "bfloat16")
for _k in range(BANKS):
    SCRATCH["ps%d" % _k] = ("psum", [128, 512], "float32")

SEMAPHORES = ["s_cw", "s_bk0", "s_bk1", "s_xb", "s_li", "s_lr", "s_xq", "s_sent", "s_out", "s_raw"]
SEMAPHORES += ["s_mix%s%d" % (k, h) for k in "cz" for h in range(2)]
SEMAPHORES += ["s_g%d%d" % (i, t) for i in range(SLOTS) for t in range(4)] + ["s_ew%d" % i for i in range(N * O)]
SEMAPHORES += ["s_h%d" % i for i in range(SLOTS)] + ["s_al%d" % s for s in range(N)]
SEMAPHORES += ["s_%s%d" % (k, i) for k in ("ac", "az", "mm", "mw", "ev") for i in range(N * O)]

PLAN = {
    "names": ["oabc", "oabc"],
    "halved": "C1",
    "load": ["sync cw", "scalar bk1", "sync bk0", "sync xb"],
    "remote": [["W o1>c:off", "L o1>a:off", "L o1>b:off", "S o0>a:off o0>o1:rest", "S o0>b:off o0>m:rest", "S o1>m:rest",
                "S a0>m:rest", "S a1>m:all", "S b0>m:all", "S b1>m:all", "S c1>m:all"],
               ["S o0>c:off", "S o0>C:off"]],
    "tensor": "o0 o1 a0 a1 m0 m1 b1 b0 A0 A1 c0 c1 B0 B1 C0 C1",
    "scalar": ["g o0 0", "g o0 12", "g o1 0123", "g a1 01", "g a1 23", "g b1 0123", "e o0", "e o1", "g c1 0123", "e a0",
               "e a1", "e m0", "e m1", "e b1", "e b0", "e A1", "e c1", "e B1", "e C1 1"],
    "vector": ["g o0 3", "a o0 0312", "x 0", "q o0", "a o1 0123", "x 1", "q o1", "r c 01", "a a1 0123", "r c 23", "q a1",
               "a b1 0123", "a c1 0", "q b1", "a c1 123", "q c1", "e A0", "e c0", "e B0", "e C0", "e C1 0"],
    "store": ["o", "a", "m", "b", "A", "c", "B", "C0", "C1"],
}


def bits(engines):
    return sum(1 << e for e in engines)


def roles(rank, cores, topo):
    chips = sorted(set(topo.chip(c) for c in cores))
    here, die = chips.index(topo.chip(cores[rank])), topo.die(cores[rank])
    role = {}
    for s, c in enumerate(cores):
        names = PLAN["names"][topo.die(c)]
        role[(names if topo.die(c) == die else "m" + names[1:].upper())[chips.index(topo.chip(c)) ^ here]] = s
    return role


def crew(rank, cores, topo):
    c = cores[rank]
    near = [k for k in topo.cores_of(c) if topo.die(k) == topo.die(c) and topo.addr(k)[2] != topo.addr(c)[2]]
    return [c] + near + [k for k in range(ALL_CORES) if topo.mates(topo.chip(k), topo.chip(c))
                         and topo.die(k) == topo.die(c) and topo.may_write(k, c)]


def tiles_of(item):
    return [item[1] if item[1] in "hpq" else int(item[1])] if len(item) > 1 else list(range(O))


def remote_steps(rank, who, cores, topo):
    role, core = roles(rank, cores, topo), crew(rank, cores, topo)[who]
    on, off = topo.engines(core, min(set(topo.cores_of(core)) - {core})), topo.engines(core, cores[role["a"]])
    rest, h = [e for e in on if e not in off], len(off) // 2
    sets = {"all": on, "off": off, "rest": rest, "off0": off[:h], "off1": off[h:], "rest0": rest[:h], "rest1": rest[h:]}
    steps = []
    for step in PLAN["remote"][who]:
        ways = []
        for way in step.split()[1:]:
            item, to = way.split(">")
            dsts, eng = to.split(":")
            ways.append((role[item[0]], tiles_of(item), [(role[d[0]], int(d[1:] or 0)) for d in dsts.split("+")], sets[eng]))
        steps += [(kind, ways) for kind in {"S": "CZ", "R": "ZC"}.get(step[0], step[0])]
    return steps


def rank_program(g, core, T, topo):
    cores = T.cores
    place = [(s, who) for s in range(N) for who in range(len(PLAN["remote"])) if crew(s, cores, topo)[who] == core]
    if not place:
        return
    r, who = place[0]
    role = roles(r, cores, topo)
    mixed = any("oh>" in step for step in PLAN["remote"][0])
    made_mix, come_mix = (role["c"], 1), (role["C"], 1)

    def tile(word):
        return role[word[0]], int(word[1])

    def kept(s):
        return topo.die(cores[s])

    def landing(s, tt, d):
        if tt == ["h"]:
            a = W + (1 - kept(s)) * H
            return (s if d[0] == s else roles(d[0], cores, topo)["C"]), a, a + H
        return s, tt[0] * W, (tt[-1] + 1) * W

    def arrival(kind, s, tt, d):
        if tt[0] in ("p", "q"):
            return "s_raw"
        k, a, _ = landing(s, tt, d)
        if tt == ["h"]:
            return "s_mix%s%d" % (kind.lower(), kept(s))
        return "s_al%d" % s if kind in "LW" else "s_a%s%d" % (kind.lower(), k * O + a // W)

    ready, slot = {}, {}
    if who == 0:
        for o in range(O):
            ready["L", r, o], ready["W", r, o] = ("s_li", 4), ("s_cw", 16)
        for op in PLAN["vector"]:
            if op[0] == "r":
                ready["L", role[op.split()[1]], 1] = ("s_lr", 4)
            if op[0] == "q":
                s, o = tile(op.split()[1])
                slot[s, o] = len(slot)
                ready["C", s, o] = ready["Z", s, o] = ("s_ac%d" % (s * O + o), 1)
        ready["C", r, "h"] = ready["Z", r, "h"] = ready["C", r, 1]
        ready["W", r, "p"] = ready["W", r, "q"] = ready["W", r, 1]
    count = {}
    for src in range(N):
        for member in range(len(PLAN["remote"])):
            for kind, ways in remote_steps(src, member, cores, topo):
                for s, tt, dsts, eng in ways:
                    if (r, who) in dsts:
                        sem = arrival(kind, s, tt, (r, who))
                        count[sem] = count.get(sem, 0) + len(eng)
                        for o in tt:
                            ready[kind, s, o] = (sem, count[sem])
    if mixed and who == 0:
        ready["W", role["c"], 1] = ("s_raw", count["s_raw"])

    seen = set()

    def once(name, q, sem, val):
        if (name, sem) not in seen:
            seen.add((name, sem))
            q.wait_ge(T.sem[sem], val)

    def view(kind, s, tt, d):
        if tt[0] in ("p", "q"):
            m, a, b = "pq".index(tt[0]), kept(s) * LC // 2, (kept(s) + 1) * LC // 2
            return T.cwl[:, 2 + m, a:b] if d == (s, 0) else T.raw[:, m, a:b]
        k, a, b = landing(s, tt, d)
        if kind == "W":
            return T.cwl[:, 2:4, :] if d == (s, 0) else T.raw[:, :, :]
        if kind == "L":
            return T["li%d" % s][:, 2 * tt[0]:2 * tt[-1] + 2, :]
        return T["w%d" % k][:, a:b].bitcast(dt.uint8) if kind == "C" else T["z%d" % k][:, a:b]

    sent = 0
    for kind, ways in remote_steps(r, who, cores, topo):
        transfers = []
        for s, tt, dsts, eng in ways:
            for o in tt:
                once("g", g, *ready[kind, s, o])
            to = [topo.addr(crew(d, cores, topo)[k]) for d, k in dsts]
            sems = set(arrival(kind, s, tt, d) for d in dsts)
            for sem in sorted(sems):
                part = [i for i, d in enumerate(dsts) if arrival(kind, s, tt, d) == sem]
                transfers.append([RemoteDMATransfer(
                    dst_ids=[DstId(rid=to[i][0], pnc=to[i][1]) for i in part], dma_engine_mask=bits(eng),
                    remote_sem=T.sem[sem], srcs=[view(kind, s, tt, (r, who))],
                    dsts=[view(kind, s, tt, dsts[i]) for i in part]), bits(eng)])
                sent += len(eng)
        while transfers:
            now, later, taken = [], [], 0
            for tr, mask in transfers:
                if mask & taken:
                    later.append([tr, mask])
                else:
                    now.append(tr)
                    taken |= mask
            g.remote_dma_fused(now, local_sem=T.sem.s_sent)
            transfers = later
    if sent:
        g.wait_ge(T.sem.s_sent, sent)
    if who:
        return

    queue = {"sync": g.sync, "scalar": g.scalar, "vector": g.vector}
    loads = {"cw": (T.cwl[:, :, :], T.cw[:, :]), "bk0": (T.bk0[:, :], T.book[:, 0:4 * K]),
             "bk1": (T.bk1[:, :], T.book[:, 4 * K:8 * K]), "xb": (T.xb[:, :], T.x[:, :])}
    for op in PLAN["load"]:
        name, what = op.split()
        queue[name].dma_start(*loads[what]).then_inc(T.sem["s_" + what], 16)

    g.vector.wait_ge(T.sem.s_cw, 16)
    for t in range(4):
        g.vector.tensor_scalar(T["li%d" % r][:, :, t * LC:(t + 1) * LC], T.cwl[:, :, :], 4.0, float(t), AluOpType.mult,
                               AluOpType.add).then_inc(T.sem.s_li, 1)

    halved = [tile(w) for w in PLAN["halved"].split()]
    jobs = []
    for w in PLAN["tensor"].split():
        jobs += [tile(w) + (k, k * W, k * W + W) for k in range(2)] if tile(w) in halved else [tile(w) + (0, 0, T_COLS)]
    gathered = {}
    for op in PLAN["scalar"] + PLAN["vector"]:
        if op[0] == "g":
            _, item, ts = op.split()
            for t in ts:
                gathered[tile(item), int(t)] = "s_g%d%s" % (slot[tile(item)], ts[0])

    def copy(q, to, src):
        return q.activation(to, src, ActivationFunctionType.Copy) if q is g.scalar else q.tensor_copy(to, src)

    for name in ("scalar", "vector"):
        q = queue[name]
        for op in PLAN[name]:
            op = op.split()
            if op[0] == "x":
                a, b = (int(op[1]) * W, int(op[1]) * W + W) if op[1:] else (0, T_COLS)
                once(name, q, "s_xb", 16)
                q.quantize_mx(T.xq[:, a:b], T.xz[:, a:b], T.xb[:, 4 * a:4 * b]).then_inc(T.sem.s_xq, (b - a) // W)
                continue
            if op[0] == "r":
                s = role[op[1]]
                once(name, q, *ready["W", s, 1])
                for t in op[2]:
                    q.tensor_scalar(T["li%d" % s][:, 2:4, int(t) * LC:(int(t) + 1) * LC], T.raw[:, :, :], 4.0, float(t), AluOpType.mult,
                                    AluOpType.add).then_inc(T.sem.s_lr, 1)
                continue
            s, o = tile(op[1])
            if op[0] == "e":
                i, part = s * O + o, int(op[2]) if op[2:] else 0
                p = [k for k, job in enumerate(jobs) if job[:3] == (s, o, part)][0]
                a, b = jobs[p][3:]
                q.wait_ge(T.sem["s_%s%d" % ("mw" if part else "mm", i)], 1)
                copy(q, T.yb[:, i * T_COLS + a:i * T_COLS + b],
                     T["ps%d" % (p % BANKS)][:, 0:b - a]).then_inc(T.sem["s_%s%d" % ("ew" if part else "ev", i)], 1)
                continue
            gb, hb, hs = T["g%d" % slot[s, o]], T["h%d" % slot[s, o]], T.sem["s_h%d" % slot[s, o]]
            if op[0] == "q":
                q.wait_ge(hs, 4)
                q.quantize_mx(T["w%d" % s][:, o * W:(o + 1) * W], T["z%d" % s][:, o * W:(o + 1) * W],
                              hb[:, 0:4 * W]).then_inc(T.sem[ready["C", s, o][0]], 1)
                continue
            ts = [int(t) for t in op[2]]
            li, at, listed = T["li%d" % s], 2 * o, ready["L", s, o]
            once(name, q, "s_bk1" if op[0] == "g" else "s_bk0", 16)
            once(name, q, *listed)
            if op[0] == "g":
                a, b = ts[0], ts[-1] + 1
                copy(q, gb[:, a * W:b * W], T.bk1[:, 0:4 * K].indirect(li[:, at + 1, a * LC:b * LC])
                     ).then_inc(T.sem[gathered[(s, o), a]], 1)
                continue
            for t in ts:
                once(name, q, gathered[(s, o), t], 1)
                q.tensor_tensor(hb[:, t:4 * W:4], T.bk0[:, 0:4 * K].indirect(li[:, at, t * LC:(t + 1) * LC]),
                                gb[:, t * W:(t + 1) * W], AluOpType.add).then_inc(hs, 1)

    g.tensor.wait_ge(T.sem.s_xq, T_COLS // W)
    for p, (s, o, part, a, b) in enumerate(jobs):
        for k, piece in ([(role["c"], "h"), (role["C"], "h")] if mixed and (s, o) == come_mix else [(s, o)]):
            once("tensor", g.tensor, *ready["C", k, piece])
            once("tensor", g.tensor, *ready["Z", k, piece])
        if p >= BANKS:
            s2, o2, part2 = jobs[p - BANKS][:3]
            g.tensor.wait_ge(T.sem["s_%s%d" % ("ew" if part2 else "ev", s2 * O + o2)], 1)
        g.tensor.matmul_mx(T["ps%d" % (p % BANKS)][:, 0:b - a], T["w%d" % s][:, o * W:(o + 1) * W],
                           T["z%d" % s][:, o * W:(o + 1) * W], T.xq[:, a:b], T.xz[:, a:b],
                           True, True).then_inc(T.sem["s_%s%d" % ("mw" if part else "mm", s * O + o)], 1)

    stores = 0
    for group in PLAN["store"]:
        for w in group.split():
            if w[0] == "@":
                g.sync.wait_ge(T.sem[ready[("C",) + tile(w[1:])][0]], 1)
        items = [(role[w[0]], o) for w in group.split() if w[0] != "@" for o in tiles_of(w)]
        blocks = sorted(s * O + o for s, o in items)
        for i in blocks:
            g.sync.wait_ge(T.sem["s_ev%d" % i], 1)
            if divmod(i, O) in halved:
                g.sync.wait_ge(T.sem["s_ew%d" % i], 1)
        a, b = blocks[0] * T_COLS, (blocks[-1] + 1) * T_COLS
        pieces = [(0, 128, a)]
        if mixed and items[0] in (made_mix, come_mix):
            halves = {s: kept(s) if items[0] == made_mix else 1 - kept(s) for s in (role["c"], role["C"])}
            pieces = [(h * H, (h + 1) * H, (s * O + 1) * T_COLS) for s, h in halves.items()]
        for p0, p1, to in pieces:
            g.sync.dma_start(T.y[p0:p1, to:to + b - a], T.yb[p0:p1, a:b]).then_inc(T.sem.s_out, 16)
            stores += 1
    g.sync.wait_ge(T.sem.s_out, 16 * stores)
